import numpy as np
import ml_dtypes


def mxq(x, axis, fmt="e4m3"):
    dtype, down = {"e4m3": (ml_dtypes.float8_e4m3fn, 7), "e5m2": (ml_dtypes.float8_e5m2, 14)}[fmt]
    v = np.moveaxis(np.asarray(x, np.float32).astype(ml_dtypes.bfloat16).astype(np.float64), axis, -1)
    blocks = v.reshape(v.shape[:-1] + (-1, 32))
    amax = np.abs(blocks).max(-1, keepdims=True)
    byte = np.maximum(np.where(amax > 0, np.frexp(amax)[1] - 1 + 127, 0) - down, 1)
    scale = np.exp2(byte - 127.0)
    codes = (blocks / scale).astype(np.float32).astype(dtype).astype(np.float64)
    return np.moveaxis((codes * scale).reshape(v.shape), -1, axis)


WIDE = False


def mx_kscale(k):
    if not WIDE:
        return np.ones(k)
    levels = np.array([10, -10, 5, -5, 0])
    if k % 512:
        return np.exp2(np.random.permutation(np.resize(levels, k // 32))).repeat(32)
    a = np.empty((k // 512, 16))
    for p in range(k // 512):
        a[p, :8] = np.random.permutation(np.resize(levels, 8))
        for g in range(8):
            far = levels[np.abs(levels - a[p, g]) >= 10]
            a[p, g + 8] = far[np.random.randint(len(far))]
    return np.exp2(a.ravel()).repeat(32)


def f64(x):
    return np.asarray(x).astype(np.float64)


def striped(idx):
    return np.tile(idx.reshape(-1, 16).T, (8, 1)).astype(np.uint16)


def unstriped(offs):
    return offs[:16].T.reshape(-1).astype(np.int64)


def striped8(idx):
    return np.concatenate([x.reshape(-1, 16).T for x in idx]).astype(np.uint16)


def runs(offs, k):
    lists = np.stack([offs[16 * r : 16 * r + 16].T.reshape(-1) for r in range(8)]).astype(np.int64)
    return lists[np.arange(k) % 512 // 64]


def pack_weight(w):
    k, n = w.shape
    w = f64(np.asarray(w, np.float32).astype(ml_dtypes.bfloat16)).reshape(k // 32, 32, n)
    amax = np.abs(w).max(1)
    byte = np.clip(np.where(amax > 0, np.frexp(amax)[1] - 1 + 127 - 7, 1), 1, 254)
    scaled = (w * np.exp2(127.0 - byte)[:, None, :]).reshape(k, n).astype(np.float32)
    words = np.ascontiguousarray(scaled.reshape(k // 512, 128, 4, n).transpose(0, 1, 3, 2)).astype(ml_dtypes.float8_e4m3fn).view(np.uint8)
    return words, np.ascontiguousarray(byte.astype(np.uint8).reshape(k // 512, 16, n))


def unpack_weight(words, scales):
    g, p, n, _ = words.shape
    vals = np.ascontiguousarray(words).view(ml_dtypes.float8_e4m3fn).astype(np.float64) * np.repeat(np.exp2(scales.astype(np.float64) - 127.0), 8, axis=1)[..., None]
    return vals.transpose(0, 1, 3, 2).reshape(g * 512, n)


E2M1 = np.array([0.0, 0.5, 1.0, 1.5, 2.0, 3.0, 4.0, 6.0, -0.0, -0.5, -1.0, -1.5, -2.0, -3.0, -4.0, -6.0])


def pack_fp4(w):
    k, n = w.shape
    w = f64(np.asarray(w, np.float32).astype(ml_dtypes.bfloat16)).reshape(k // 32, 32, n)
    amax = np.abs(w).max(1)
    mant, ex = np.frexp(amax / 6.0)
    byte = np.clip(np.where(amax > 0, np.where(mant > 0.5, ex, ex - 1) + 127, 1), 1, 254)
    scaled = (w * np.exp2(127.0 - byte)[:, None, :]).reshape(k, n).astype(np.float32)
    c = np.ascontiguousarray(scaled.reshape(k // 512, 128, 4, n).transpose(0, 1, 3, 2)).astype(ml_dtypes.float4_e2m1fn).view(np.uint8) & 0xF
    words = (c[..., 0::2] | (c[..., 1::2] << 4)).reshape(k // 512, 128, 2 * n)
    return np.ascontiguousarray(words), np.ascontiguousarray(byte.astype(np.uint8).reshape(k // 512, 16, n))


def unpack_fp4(words, scales):
    g, _, n = scales.shape
    words = np.ascontiguousarray(words).reshape(g, 128, n, 2)
    nib = np.empty((g, 128, n, 4), np.uint8)
    nib[..., 0::2] = words & 0xF
    nib[..., 1::2] = words >> 4
    vals = E2M1[nib] * np.repeat(np.exp2(scales.astype(np.float64) - 127.0), 8, axis=1)[..., None]
    return vals.transpose(0, 1, 3, 2).reshape(g * 512, n)


def sigmoid(v):
    return 1.0 / (1.0 + np.exp(-np.maximum(v, -700.0)))

def planes(y):
    n, m = y.shape
    v = y.astype(np.float32).astype(ml_dtypes.bfloat16).astype(np.float64).reshape(n // 32, 32, m)
    top = np.abs(v).max(1)
    byte = np.clip(np.where(top > 0, np.frexp(top)[1] - 1 + 127 - 7, 1), 1, 254)
    codes = (v * np.exp2(127.0 - byte)[:, None, :]).reshape(n, m).astype(np.float32).astype(ml_dtypes.float8_e4m3fn).view(np.uint8)
    words = codes.reshape(n // 512, 128, 4, m).transpose(0, 1, 3, 2)
    return np.ascontiguousarray(words), np.ascontiguousarray(byte.astype(np.uint8).reshape(n // 512, 16, m))


K, T, S, N, H = 512, 2048, 512, 512, 512


def setup_inputs():
    n = np.random.standard_normal
    s = mx_kscale(K)[:, None]
    u = mx_kscale(H)
    packed_xT = pack_weight(n((K, T)) * s)
    packed_w1 = pack_fp4(n((K, H)) / np.sqrt(K) / s)
    packed_w2 = pack_fp4(n((K, H)) / np.sqrt(K) / s)
    packed_w3 = pack_fp4(n((H, N)) / np.sqrt(H) / u[:, None])
    return {
        "x_words": packed_xT[0],
        "x_scales": packed_xT[1],
        "w1_words": packed_w1[0],
        "w1_scales": packed_w1[1],
        "w2_words": packed_w2[0],
        "w2_scales": packed_w2[1],
        "gn": (np.random.uniform(0.5, 1.5, (H, 1)) * u[:, None]).astype(np.float32),
        "w3_words": packed_w3[0],
        "w3_scales": packed_w3[1],
        "offs": striped(np.random.permutation(T)[:S]),
        "two": striped(np.random.permutation(T)[:S]),
        "b1": striped8(np.stack([np.random.permutation(S) for _ in range(8)])),
        "b3": striped8(np.stack([np.random.permutation(S) for _ in range(8)])),
        "b4": striped8(np.stack([np.random.permutation(S) for _ in range(8)])),
    }


def reference(x_words, x_scales, w1_words, w1_scales, w2_words, w2_scales, gn, w3_words, w3_scales, offs, two, b1, b3, b4):
    x_two = unpack_weight(x_words, x_scales)[:, unstriped(two)]
    c = sigmoid(unpack_fp4(w2_words, w2_scales).T @ x_two)
    v1 = c[np.arange(H)[:, None], runs(b1, H)]
    xq = unpack_weight(x_words, x_scales)[:, unstriped(offs)]
    y = unpack_fp4(w1_words, w1_scales).T @ xq
    v3 = c[np.arange(H)[:, None], runs(b3, H)]
    v4 = c[np.arange(H)[:, None], runs(b4, H)]
    z = f64(gn) * ((v1 * (y[np.arange(H)[:, None], runs(b1, H)]) + v3 * (y[np.arange(H)[:, None], runs(b3, H)]) + v4 * (y[np.arange(H)[:, None], runs(b4, H)])) / (v1 + v3 + v4))
    out_0 = unpack_fp4(w3_words, w3_scales).T @ mxq(z, 0, "e4m3")
    return (out_0,) + planes(out_0)

@@ -1,0 +1,231 @@
+from contextlib import ExitStack
+
+import concourse.mybir as mybir
+from concourse.masks import make_identity
+
+K, T, S, N, H = 512, 2048, 512, 512, 512
+FLOPS = 2 * K * H * S * 2 + 2 * H * N * S
+
+F32 = mybir.dt.float32
+BF16 = mybir.dt.bfloat16
+I32 = mybir.dt.int32
+U32 = mybir.dt.uint32
+U16 = mybir.dt.uint16
+U8 = mybir.dt.uint8
+FP8X4 = mybir.dt.float8_e4m3fn_x4
+FP4X4 = mybir.dt.float4_e2m1fn_x4
+ACT = mybir.ActivationFunctionType
+MULT = mybir.AluOpType.mult
+
+P = 128
+TILES = 4
+BLOCKS = S // P
+HALF = S // 2
+VECTOR_DEN_TILE = 3
+
+
+def tile_picked_vwap3_none_po_kernel(
+    tc, x_words, x_scales, w1_words, w1_scales, w2_words, w2_scales, gn, w3_words, w3_scales,
+    offs, two, b1, b3, b4, out_0, out_1, out_2,
+):
+    nc = tc.nc
+    with ExitStack() as ctx:
+        lists = ctx.enter_context(tc.tile_pool(name="lists", bufs=1))
+        sb = ctx.enter_context(tc.tile_pool(name="sb", bufs=1))
+        ps = ctx.enter_context(tc.psum_pool(name="ps", bufs=1))
+
+        def sbuf(name, shape, dtype):
+            return sb.tile(shape, dtype, name=name, align_bytes=64)
+
+        def bank(b, name):
+            return ps.tile([P, 512], F32, name=name, tag="bank%d" % b)
+
+        def load_list(name, src):
+            held = lists.tile([P, S // 16], U16, name=name)
+            nc.sync.dma_start(held[:], src)
+            return held
+
+        def load_scale_rows(plane, scales):
+            for q in range(4):
+                nc.sync.dma_start(
+                    out=plane[32 * q : 32 * q + 4, :].bitcast(I32), in_=scales[0, 4 * q : 4 * q + 4, :].bitcast(I32)
+                )
+
+        xw = sbuf("xw", [P, T], I32)
+        xs = sbuf("xs", [P, T], U8)
+        raw_w = [sbuf("raw_w%d" % i, [P, 2 * H], U8) for i in range(2)]
+        raw_s = [sbuf("raw_s%d" % i, [P, H], U8) for i in range(2)]
+        gn_rows = sbuf("gn_rows", [P, P], F32)
+        ident = sbuf("ident", [P, P], F32)
+
+        nc.vector.memset(xs[:].bitcast(I32), 0)
+        nc.vector.memset(raw_s[1][:].bitcast(I32), 0)
+        nc.vector.memset(raw_s[0][:].bitcast(I32), 0)
+        nc.vector.memset(gn_rows[:], 0.0)
+        make_identity(nc, ident[:])
+
+        two_t = load_list("two_t", two)
+        offs_t = load_list("offs_t", offs)
+        picks = [load_list(name, src) for name, src in (("b1_t", b1), ("b3_t", b3), ("b4_t", b4))]
+        nc.sync.dma_start(out=xw[:], in_=x_words[0].rearrange("p c r -> p (c r)").bitcast(I32))
+        for i, words in ((1, w2_words), (0, w1_words)):
+            nc.sync.dma_start(out=raw_w[i][:].bitcast(I32), in_=words[0].bitcast(I32))
+        load_scale_rows(xs, x_scales)
+        load_scale_rows(raw_s[1], w2_scales)
+        load_scale_rows(raw_s[0], w1_scales)
+        nc.sync.dma_start(
+            out=gn_rows[0:TILES, :].rearrange("t (g i) -> t g i", i=16),
+            in_=gn.rearrange("(g t i) o -> t g (i o)", t=TILES, i=16),
+        )
+
+        w = [sbuf("w%d" % i, [P, 2 * H], U8) for i in range(3)]
+        ws = [sbuf("ws%d" % i, [P, H], U8) for i in range(3)]
+
+        def deal_by_runs(i):
+            for dst, src, words in ((w[i], raw_w[i], 8), (ws[i], raw_s[i], 4)):
+                nc.vector.tensor_copy(
+                    out=dst[:].bitcast(I32).rearrange("p (t g k) -> p t g k", t=TILES, k=words),
+                    in_=src[:].bitcast(I32).rearrange("p (g t k) -> p t g k", t=TILES, k=words),
+                )
+
+        def pick_scales(name, index):
+            got = sbuf(name, [P, S], U8)
+            nc.vector.tensor_copy(out=got[:], in_=xs[:].indirect(index[:]))
+            return got
+
+        def pick_words(name, index):
+            got = sbuf(name, [P, S], U32)
+            nc.vector.tensor_copy(out=got[:], in_=xw[:].bitcast(U32).indirect(index[:]))
+            return got
+
+        def product(out, i, t, codes, scales):
+            nc.tensor.matmul_mx(
+                out=out,
+                lhsT=w[i][:, 2 * P * t : 2 * P * (t + 1)].bitcast(FP4X4),
+                lhsT_scale=ws[i][:, P * t : P * (t + 1)],
+                rhs=codes.bitcast(FP8X4),
+                rhs_scale=scales,
+                start=True,
+                stop=True,
+            )
+
+        two_w = pick_words("two_w", two_t)
+        two_s = pick_scales("two_s", two_t)
+        deal_by_runs(1)
+        nc.sync.dma_start(out=raw_w[1][:].bitcast(I32), in_=w3_words[0].bitcast(I32))
+        load_scale_rows(raw_s[1], w3_scales)
+        offs_w = pick_words("offs_w", offs_t)
+        offs_s = pick_scales("offs_s", offs_t)
+        deal_by_runs(0)
+
+        logit, volume, traded = [], [], []
+        for t in range(TILES):
+            u_bank = bank(t, "u_bank%d" % t)
+            product(u_bank[:], 1, t, two_w[:], two_s[:])
+            c = sbuf("volume%d" % t, [P, S], F32)
+            nc.scalar.activation(c[:], u_bank[:], ACT.Sigmoid)
+            volume.append(c)
+            if t != VECTOR_DEN_TILE:
+                u = sbuf("logit%d" % t, [P, S], F32)
+                nc.scalar.copy(u[:], u_bank[:])
+                logit.append(u)
+        gn_bank = bank(0, "gn_bank")
+        nc.tensor.transpose(gn_bank[:, 0:P], gn_rows[:], ident[:])
+        gain = sbuf("gain", [P, TILES], F32)
+        nc.vector.tensor_copy(out=gain[:], in_=gn_bank[:, 0:TILES])
+
+        for t in range(TILES):
+            y_bank = bank(4 + t, "y_bank%d" % t)
+            product(y_bank[:], 0, t, offs_w[:], offs_s[:])
+            cy = sbuf("traded%d" % t, [P, S], F32)
+            nc.vector.scalar_tensor_tensor(cy[:], y_bank[:], gain[:, t : t + 1], volume[t][:], MULT, MULT)
+            traded.append(cy)
+
+        nc.vector.tensor_copy(
+            out=w[2][:].rearrange("p (t m b) -> p t m b", t=TILES, b=2),
+            in_=raw_w[1][:].rearrange("p (m t b) -> p t m b", t=TILES, b=2),
+        )
+        nc.vector.tensor_copy(
+            out=ws[2][:].rearrange("p (t m) -> p t m", t=TILES),
+            in_=raw_s[1][:].rearrange("p (m t) -> p t m", t=TILES),
+        )
+
+        den = [bank(jb, "den%d" % jb) for jb in range(BLOCKS)]
+        num = [bank(4 + jb, "num%d" % jb) for jb in range(BLOCKS)]
+
+        def add_turned(banks, h, t, got):
+            for jb in (2 * h, 2 * h + 1):
+                for l in range(3):
+                    nc.tensor.matmul(
+                        banks[jb][:, P * t : P * (t + 1)],
+                        got[l][:, P * (jb % 2) : P * (jb % 2 + 1)],
+                        ident[:],
+                        start=(l == 0),
+                        stop=(l == 2),
+                        is_transpose=True,
+                    )
+
+        for h in range(2):
+            for t in range(TILES):
+                got_den, got_num = [], []
+                for l in range(3):
+                    index = picks[l][:, 16 * h : 16 * (h + 1)]
+                    g = sbuf("den_%d_%d_%d" % (h, t, l), [P, HALF], F32)
+                    if t == VECTOR_DEN_TILE:
+                        nc.vector.tensor_copy(out=g[:], in_=volume[t][:].indirect(index))
+                    else:
+                        nc.scalar.activation(g[:], logit[t][:].indirect(index), ACT.Sigmoid)
+                    got_den.append(g)
+                for l in range(3):
+                    index = picks[l][:, 16 * h : 16 * (h + 1)]
+                    g = sbuf("num_%d_%d_%d" % (h, t, l), [P, HALF], F32)
+                    nc.vector.tensor_copy(out=g[:], in_=traded[t][:].indirect(index))
+                    got_num.append(g)
+                add_turned(den, h, t, got_den)
+                add_turned(num, h, t, got_num)
+
+        out_words = sbuf("out_words", [P, S], I32)
+        out_scales = sbuf("out_scales", [P, S], U8)
+        out_rows = out_0.rearrange("(p t) j -> p t j", t=TILES)
+        out_codes = out_1[0].rearrange("p c r -> p (c r)").bitcast(I32)
+
+        def in_feature_order(b):
+            return b[:].rearrange("j (t g i) -> j g t i", t=TILES, i=16)
+
+        def as_runs(tile):
+            return tile[:].rearrange("j (g t i) -> j g t i", t=TILES, i=16)
+
+        for jb in range(BLOCKS):
+            cols = slice(P * jb, P * (jb + 1))
+            root = sbuf("root%d" % jb, [P, H], F32)
+            nc.scalar.activation(as_runs(root), in_feature_order(den[jb]), ACT.Abs_reciprocal_sqrt)
+            inv = sbuf("inv%d" % jb, [P, H], F32)
+            nc.scalar.activation(inv[:], root[:], ACT.Square)
+            z_t = sbuf("z_t%d" % jb, [P, H], BF16)
+            nc.vector.tensor_tensor(as_runs(z_t), in_feature_order(num[jb]), as_runs(inv), MULT)
+            z_bank = bank(jb, "z_bank%d" % jb)
+            for u in range(2):
+                nc.tensor.transpose(z_bank[:, P * u : P * (u + 1)], z_t[:].bitcast(F32)[:, u : H // 2 : 2], ident[:])
+            z = sbuf("z%d" % jb, [P, 4 * P], BF16)
+            nc.scalar.copy(
+                z[:].bitcast(F32).rearrange("p (j u) -> p j u", u=2),
+                z_bank[:, 0 : 2 * P].rearrange("p (u j) -> p j u", u=2),
+            )
+            z_words = sbuf("z_words%d" % jb, [P, P], U32)
+            z_scales = sbuf("z_scales%d" % jb, [P, P], U8)
+            nc.vector.quantize_mx(out=z_words[:].bitcast(FP8X4), scales=z_scales[:], in_=z[:])
+            o_bank = bank(4 + jb, "o_bank%d" % jb)
+            for t in range(TILES):
+                product(o_bank[:, P * t : P * (t + 1)], 2, t, z_words[:], z_scales[:])
+            o = sbuf("o%d" % jb, [P, TILES, P], F32)
+            nc.scalar.copy(o[:].rearrange("p t j -> p (t j)"), o_bank[:])
+            nc.sync.dma_start(out=out_rows[:, :, cols], in_=o[:])
+            o16 = sbuf("o16_%d" % jb, [P, P, TILES], BF16)
+            nc.vector.tensor_copy(out=o16[:], in_=o[:].rearrange("p t j -> p j t"))
+            nc.vector.quantize_mx(
+                out=out_words[:, cols].bitcast(FP8X4), scales=out_scales[:, cols], in_=o16[:].rearrange("p j t -> p (j t)")
+            )
+            nc.sync.dma_start(out=out_codes[:, cols], in_=out_words[:, cols])
+        for q in range(4):
+            queue = nc.scalar if q % 2 else nc.sync
+            queue.dma_start(out=out_2[0, 4 * q : 4 * q + 4, :].bitcast(I32), in_=out_scales[32 * q : 32 * q + 4, :].bitcast(I32))

@@ -34,8 +34,8 @@ def tile_picked_vwap3_none_po_kernel(
         sb = ctx.enter_context(tc.tile_pool(name="sb", bufs=1))
         ps = ctx.enter_context(tc.psum_pool(name="ps", bufs=1))
 
-        def sbuf(name, shape, dtype):
-            return sb.tile(shape, dtype, name=name, align_bytes=64)
+        def sbuf(name, shape, dtype, slot=None):
+            return sb.tile(shape, dtype, name=name, tag=slot or name, align_bytes=64)
 
         def bank(b, name):
             return ps.tile([P, 512], F32, name=name, tag="bank%d" % b)
@@ -45,9 +45,9 @@ def tile_picked_vwap3_none_po_kernel(
             nc.sync.dma_start(held[:], src)
             return held
 
-        def load_scale_rows(plane, scales):
+        def load_scale_rows(plane, scales, queue):
             for q in range(4):
-                nc.sync.dma_start(
+                queue.dma_start(
                     out=plane[32 * q : 32 * q + 4, :].bitcast(I32), in_=scales[0, 4 * q : 4 * q + 4, :].bitcast(I32)
                 )
 
@@ -61,35 +61,40 @@ def tile_picked_vwap3_none_po_kernel(
         nc.vector.memset(xs[:].bitcast(I32), 0)
         nc.vector.memset(raw_s[1][:].bitcast(I32), 0)
         nc.vector.memset(raw_s[0][:].bitcast(I32), 0)
-        nc.vector.memset(gn_rows[:], 0.0)
-        make_identity(nc, ident[:])
-
-        two_t = load_list("two_t", two)
-        offs_t = load_list("offs_t", offs)
-        picks = [load_list(name, src) for name, src in (("b1_t", b1), ("b3_t", b3), ("b4_t", b4))]
-        nc.sync.dma_start(out=xw[:], in_=x_words[0].rearrange("p c r -> p (c r)").bitcast(I32))
-        for i, words in ((1, w2_words), (0, w1_words)):
-            nc.sync.dma_start(out=raw_w[i][:].bitcast(I32), in_=words[0].bitcast(I32))
-        load_scale_rows(xs, x_scales)
-        load_scale_rows(raw_s[1], w2_scales)
-        load_scale_rows(raw_s[0], w1_scales)
-        nc.sync.dma_start(
+        nc.gpsimd.memset(gn_rows[:], 0.0)
+        nc.gpsimd.dma_start(
             out=gn_rows[0:TILES, :].rearrange("t (g i) -> t g i", i=16),
             in_=gn.rearrange("(g t i) o -> t g (i o)", t=TILES, i=16),
         )
+        make_identity(nc, ident[:])
+
+        nc.scalar.dma_start(out=xw[:], in_=x_words[0].rearrange("p c r -> p (c r)").bitcast(I32))
+        two_t = load_list("two_t", two)
+        offs_t = load_list("offs_t", offs)
+        nc.sync.dma_start(out=raw_w[1][:].bitcast(I32), in_=w2_words[0].bitcast(I32))
+        load_scale_rows(xs, x_scales, nc.sync)
+        load_scale_rows(raw_s[1], w2_scales, nc.sync)
+        nc.sync.dma_start(out=raw_w[0][:].bitcast(I32), in_=w1_words[0].bitcast(I32))
+        load_scale_rows(raw_s[0], w1_scales, nc.sync)
+        picks = [load_list(name, src) for name, src in (("b1_t", b1), ("b3_t", b3), ("b4_t", b4))]
+
+        gn_bank = bank(0, "gn_bank")
+        nc.tensor.transpose(gn_bank[:, 0:P], gn_rows[:], ident[:])
+        gain = sbuf("gain", [P, TILES], F32)
+        nc.scalar.copy(gain[:], gn_bank[:, 0:TILES])
 
         w = [sbuf("w%d" % i, [P, 2 * H], U8) for i in range(3)]
-        ws = [sbuf("ws%d" % i, [P, H], U8) for i in range(3)]
+        ws2_first = sbuf("ws2_first", [P, P], U8)
+        ws2_rest = sbuf("ws2_rest", [P, H - P], U8)
 
-        def deal_by_runs(i):
-            for dst, src, words in ((w[i], raw_w[i], 8), (ws[i], raw_s[i], 4)):
-                nc.vector.tensor_copy(
-                    out=dst[:].bitcast(I32).rearrange("p (t g k) -> p t g k", t=TILES, k=words),
-                    in_=src[:].bitcast(I32).rearrange("p (g t k) -> p t g k", t=TILES, k=words),
-                )
+        def deal_by_runs(dst, src, words, t0, t1):
+            nc.vector.tensor_copy(
+                out=dst.bitcast(I32).rearrange("p (t g k) -> p t g k", t=t1 - t0, k=words),
+                in_=src[:].bitcast(I32).rearrange("p (g t k) -> p t g k", t=TILES, k=words)[:, t0:t1],
+            )
 
-        def pick_scales(name, index):
-            got = sbuf(name, [P, S], U8)
+        def pick_scales(name, index, slot=None):
+            got = sbuf(name, [P, S], U8, slot)
             nc.vector.tensor_copy(out=got[:], in_=xs[:].indirect(index[:]))
             return got
 
@@ -98,91 +103,106 @@ def tile_picked_vwap3_none_po_kernel(
             nc.vector.tensor_copy(out=got[:], in_=xw[:].bitcast(U32).indirect(index[:]))
             return got
 
+        def weight_scales(i, t):
+            if i != 1:
+                return ws[i][:, P * t : P * (t + 1)]
+            return ws2_first[:] if t == 0 else ws2_rest[:, P * (t - 1) : P * t]
+
         def product(out, i, t, codes, scales):
             nc.tensor.matmul_mx(
                 out=out,
                 lhsT=w[i][:, 2 * P * t : 2 * P * (t + 1)].bitcast(FP4X4),
-                lhsT_scale=ws[i][:, P * t : P * (t + 1)],
+                lhsT_scale=weight_scales(i, t),
                 rhs=codes.bitcast(FP8X4),
                 rhs_scale=scales,
                 start=True,
                 stop=True,
             )
 
-        two_w = pick_words("two_w", two_t)
         two_s = pick_scales("two_s", two_t)
-        deal_by_runs(1)
-        nc.sync.dma_start(out=raw_w[1][:].bitcast(I32), in_=w3_words[0].bitcast(I32))
-        load_scale_rows(raw_s[1], w3_scales)
-        offs_w = pick_words("offs_w", offs_t)
+        two_w = pick_words("two_w", two_t)
+        deal_by_runs(w[1][:], raw_w[1], 8, 0, TILES)
+        deal_by_runs(ws2_first[:], raw_s[1], 4, 0, 1)
+        deal_by_runs(ws2_rest[:], raw_s[1], 4, 1, TILES)
         offs_s = pick_scales("offs_s", offs_t)
-        deal_by_runs(0)
+        offs_w = pick_words("offs_w", offs_t)
+        deal_by_runs(w[0][:], raw_w[0], 8, 0, TILES)
+        ws = {2: sbuf("ws3", [P, H], U8)}
 
-        logit, volume, traded = [], [], []
-        for t in range(TILES):
+        den_window = [sbuf("den_window%d" % t, [P, 2 * S], F32) for t in range(TILES)]
+        traded = [sbuf("traded%d" % t, [P, 2 * S], F32) for t in range(TILES)]
+
+        def volume(t):
+            return den_window[t][:, 0:S] if t == VECTOR_DEN_TILE else den_window[t][:, S : 2 * S]
+
+        def project_volumes(t):
             u_bank = bank(t, "u_bank%d" % t)
             product(u_bank[:], 1, t, two_w[:], two_s[:])
-            c = sbuf("volume%d" % t, [P, S], F32)
-            nc.scalar.activation(c[:], u_bank[:], ACT.Sigmoid)
-            volume.append(c)
+            nc.scalar.activation(volume(t), u_bank[:], ACT.Sigmoid)
             if t != VECTOR_DEN_TILE:
-                u = sbuf("logit%d" % t, [P, S], F32)
-                nc.scalar.copy(u[:], u_bank[:])
-                logit.append(u)
-        gn_bank = bank(0, "gn_bank")
-        nc.tensor.transpose(gn_bank[:, 0:P], gn_rows[:], ident[:])
-        gain = sbuf("gain", [P, TILES], F32)
-        nc.vector.tensor_copy(out=gain[:], in_=gn_bank[:, 0:TILES])
+                nc.scalar.copy(den_window[t][:, 0:S], u_bank[:])
 
-        for t in range(TILES):
+        def project_prices(t):
             y_bank = bank(4 + t, "y_bank%d" % t)
             product(y_bank[:], 0, t, offs_w[:], offs_s[:])
-            cy = sbuf("traded%d" % t, [P, S], F32)
-            nc.vector.scalar_tensor_tensor(cy[:], y_bank[:], gain[:, t : t + 1], volume[t][:], MULT, MULT)
-            traded.append(cy)
+            nc.vector.scalar_tensor_tensor(traded[t][:, 0:S], y_bank[:], gain[:, t : t + 1], volume(t), MULT, MULT)
+
+        project_volumes(0)
+        ws.setdefault(0, sbuf("ws1", [P, H], U8, "ws2_first"))
+        deal_by_runs(ws[0][:], raw_s[0], 4, 0, TILES)
+        nc.sync.dma_start(out=raw_w[0][:].bitcast(I32), in_=w3_words[0].bitcast(I32))
+        load_scale_rows(raw_s[0], w3_scales, nc.sync)
+        for t in range(1, TILES):
+            project_volumes(t)
+            project_prices(t - 1)
+        project_prices(TILES - 1)
 
         nc.vector.tensor_copy(
             out=w[2][:].rearrange("p (t m b) -> p t m b", t=TILES, b=2),
-            in_=raw_w[1][:].rearrange("p (m t b) -> p t m b", t=TILES, b=2),
+            in_=raw_w[0][:].rearrange("p (m t b) -> p t m b", t=TILES, b=2),
         )
         nc.vector.tensor_copy(
             out=ws[2][:].rearrange("p (t m) -> p t m", t=TILES),
-            in_=raw_s[1][:].rearrange("p (m t) -> p t m", t=TILES),
+            in_=raw_s[0][:].rearrange("p (m t) -> p t m", t=TILES),
         )
 
         den = [bank(jb, "den%d" % jb) for jb in range(BLOCKS)]
         num = [bank(4 + jb, "num%d" % jb) for jb in range(BLOCKS)]
 
-        def add_turned(banks, h, t, got):
-            for jb in (2 * h, 2 * h + 1):
+        def add_turned(banks, t, got, blocks):
+            for n, jb in enumerate(blocks):
                 for l in range(3):
                     nc.tensor.matmul(
                         banks[jb][:, P * t : P * (t + 1)],
-                        got[l][:, P * (jb % 2) : P * (jb % 2 + 1)],
+                        got[:, l, P * n : P * (n + 1)],
                         ident[:],
                         start=(l == 0),
                         stop=(l == 2),
                         is_transpose=True,
                     )
 
-        for h in range(2):
-            for t in range(TILES):
-                got_den, got_num = [], []
-                for l in range(3):
-                    index = picks[l][:, 16 * h : 16 * (h + 1)]
-                    g = sbuf("den_%d_%d_%d" % (h, t, l), [P, HALF], F32)
-                    if t == VECTOR_DEN_TILE:
-                        nc.vector.tensor_copy(out=g[:], in_=volume[t][:].indirect(index))
-                    else:
-                        nc.scalar.activation(g[:], logit[t][:].indirect(index), ACT.Sigmoid)
-                    got_den.append(g)
-                for l in range(3):
-                    index = picks[l][:, 16 * h : 16 * (h + 1)]
-                    g = sbuf("num_%d_%d_%d" % (h, t, l), [P, HALF], F32)
-                    nc.vector.tensor_copy(out=g[:], in_=traded[t][:].indirect(index))
-                    got_num.append(g)
-                add_turned(den, h, t, got_den)
-                add_turned(num, h, t, got_num)
+        def pick_volumes(t):
+            got = sbuf("den_%d" % t, [P, 3, S], F32)
+            for l in range(3):
+                if t == VECTOR_DEN_TILE:
+                    nc.vector.tensor_copy(out=got[:, l, :], in_=den_window[t][:].indirect(picks[l][:]))
+                else:
+                    nc.scalar.activation(got[:, l, :], den_window[t][:].indirect(picks[l][:]), ACT.Sigmoid)
+            add_turned(den, t, got, range(BLOCKS))
+
+        def pick_traded(t, blocks, slot=None):
+            got = sbuf("num_%d_%d" % (t, blocks[0]), [P, 3, P * len(blocks)], F32, slot)
+            for l in range(3):
+                index = picks[l][:, 8 * blocks[0] : 8 * (blocks[-1] + 1)]
+                nc.vector.tensor_copy(out=got[:, l, :], in_=traded[t][:].indirect(index))
+            add_turned(num, t, got, blocks)
+
+        pick_traded(0, (0, 1, 2, 3))
+        for t in (0, VECTOR_DEN_TILE, 1, 2):
+            pick_volumes(t)
+        pick_traded(1, (0, 1, 2, 3))
+        pick_traded(2, (0, 1))
+        pick_traded(3, (0, 1))
 
         out_words = sbuf("out_words", [P, S], I32)
         out_scales = sbuf("out_scales", [P, S], U8)
@@ -203,6 +223,8 @@ def tile_picked_vwap3_none_po_kernel(
             nc.scalar.activation(inv[:], root[:], ACT.Square)
             z_t = sbuf("z_t%d" % jb, [P, H], BF16)
             nc.vector.tensor_tensor(as_runs(z_t), in_feature_order(num[jb]), as_runs(inv), MULT)
+            if jb < 2:
+                pick_traded(2 + jb, (2, 3), "inv%d" % jb)
             z_bank = bank(jb, "z_bank%d" % jb)
             for u in range(2):
                 nc.tensor.transpose(z_bank[:, P * u : P * (u + 1)], z_t[:].bitcast(F32)[:, u : H // 2 : 2], ident[:])

@@ -47,7 +47,7 @@ def tile_picked_vwap3_none_po_kernel(
 
         def load_scale_rows(plane, scales, queue):
             for q in range(4):
-                queue.dma_start(
+                (queue if q % 2 else nc.sync).dma_start(
                     out=plane[32 * q : 32 * q + 4, :].bitcast(I32), in_=scales[0, 4 * q : 4 * q + 4, :].bitcast(I32)
                 )
 
@@ -59,31 +59,32 @@ def tile_picked_vwap3_none_po_kernel(
         ident = sbuf("ident", [P, P], F32)
 
         nc.vector.memset(xs[:].bitcast(I32), 0)
+        nc.vector.memset(gn_rows[:], 0.0)
         nc.vector.memset(raw_s[1][:].bitcast(I32), 0)
         nc.vector.memset(raw_s[0][:].bitcast(I32), 0)
-        nc.gpsimd.memset(gn_rows[:], 0.0)
-        nc.gpsimd.dma_start(
-            out=gn_rows[0:TILES, :].rearrange("t (g i) -> t g i", i=16),
-            in_=gn.rearrange("(g t i) o -> t g (i o)", t=TILES, i=16),
-        )
         make_identity(nc, ident[:])
 
-        nc.scalar.dma_start(out=xw[:], in_=x_words[0].rearrange("p c r -> p (c r)").bitcast(I32))
         two_t = load_list("two_t", two)
         offs_t = load_list("offs_t", offs)
         nc.sync.dma_start(out=raw_w[1][:].bitcast(I32), in_=w2_words[0].bitcast(I32))
         load_scale_rows(xs, x_scales, nc.sync)
+        nc.sync.dma_start(out=xw[:], in_=x_words[0].rearrange("p c r -> p (c r)").bitcast(I32))
+        nc.sync.dma_start(
+            out=gn_rows[0:TILES, :].rearrange("t (g i) -> t g i", i=16),
+            in_=gn.rearrange("(g t i) o -> t g (i o)", t=TILES, i=16),
+        )
         load_scale_rows(raw_s[1], w2_scales, nc.sync)
         nc.sync.dma_start(out=raw_w[0][:].bitcast(I32), in_=w1_words[0].bitcast(I32))
         load_scale_rows(raw_s[0], w1_scales, nc.sync)
         picks = [load_list(name, src) for name, src in (("b1_t", b1), ("b3_t", b3), ("b4_t", b4))]
 
-        gn_bank = bank(0, "gn_bank")
+        gn_bank = bank(7, "gn_bank")
         nc.tensor.transpose(gn_bank[:, 0:P], gn_rows[:], ident[:])
         gain = sbuf("gain", [P, TILES], F32)
-        nc.scalar.copy(gain[:], gn_bank[:, 0:TILES])
+        nc.vector.tensor_copy(out=gain[:], in_=gn_bank[:, 0:TILES])
 
-        w = [sbuf("w%d" % i, [P, 2 * H], U8) for i in range(3)]
+        w2_first = sbuf("w2_first", [P, 2 * P], U8)
+        w2_rest = sbuf("w2_rest", [P, 2 * (H - P)], U8)
         ws2_first = sbuf("ws2_first", [P, P], U8)
         ws2_rest = sbuf("ws2_rest", [P, H - P], U8)
 
@@ -98,8 +99,8 @@ def tile_picked_vwap3_none_po_kernel(
             nc.vector.tensor_copy(out=got[:], in_=xs[:].indirect(index[:]))
             return got
 
-        def pick_words(name, index):
-            got = sbuf(name, [P, S], U32)
+        def pick_words(name, index, slot=None):
+            got = sbuf(name, [P, S], U32, slot)
             nc.vector.tensor_copy(out=got[:], in_=xw[:].bitcast(U32).indirect(index[:]))
             return got
 
@@ -108,10 +109,15 @@ def tile_picked_vwap3_none_po_kernel(
                 return ws[i][:, P * t : P * (t + 1)]
             return ws2_first[:] if t == 0 else ws2_rest[:, P * (t - 1) : P * t]
 
+        def weight_words(i, t):
+            if i != 1:
+                return w[i][:, 2 * P * t : 2 * P * (t + 1)]
+            return w2_first[:] if t == 0 else w2_rest[:, 2 * P * (t - 1) : 2 * P * t]
+
         def product(out, i, t, codes, scales):
             nc.tensor.matmul_mx(
                 out=out,
-                lhsT=w[i][:, 2 * P * t : 2 * P * (t + 1)].bitcast(FP4X4),
+                lhsT=weight_words(i, t).bitcast(FP4X4),
                 lhsT_scale=weight_scales(i, t),
                 rhs=codes.bitcast(FP8X4),
                 rhs_scale=scales,
@@ -121,26 +127,28 @@ def tile_picked_vwap3_none_po_kernel(
 
         two_s = pick_scales("two_s", two_t)
         two_w = pick_words("two_w", two_t)
-        deal_by_runs(w[1][:], raw_w[1], 8, 0, TILES)
+        deal_by_runs(w2_first[:], raw_w[1], 8, 0, 1)
+        deal_by_runs(w2_rest[:], raw_w[1], 8, 1, TILES)
         deal_by_runs(ws2_first[:], raw_s[1], 4, 0, 1)
         deal_by_runs(ws2_rest[:], raw_s[1], 4, 1, TILES)
         offs_s = pick_scales("offs_s", offs_t)
-        offs_w = pick_words("offs_w", offs_t)
-        deal_by_runs(w[0][:], raw_w[0], 8, 0, TILES)
+        offs_w = pick_words("offs_w", offs_t, "raw_s1")
+        nc.sync.dma_start(out=raw_w[1][:].bitcast(I32), in_=w3_words[0].bitcast(I32))
+        w = {}
         ws = {2: sbuf("ws3", [P, H], U8)}
 
-        den_window = [sbuf("den_window%d" % t, [P, 2 * S], F32) for t in range(TILES)]
+        logit = [sbuf("logit%d" % t, [P, 2 * S], F32) for t in range(TILES)]
+        volumes = [sbuf("volume%d" % t, [P, 2 * S], F32) for t in range(TILES)]
         traded = [sbuf("traded%d" % t, [P, 2 * S], F32) for t in range(TILES)]
 
         def volume(t):
-            return den_window[t][:, 0:S] if t == VECTOR_DEN_TILE else den_window[t][:, S : 2 * S]
+            return volumes[t][:, 0:S]
 
         def project_volumes(t):
-            u_bank = bank(t, "u_bank%d" % t)
+            u_bank = bank(t % 2, "u_bank%d" % t)
             product(u_bank[:], 1, t, two_w[:], two_s[:])
             nc.scalar.activation(volume(t), u_bank[:], ACT.Sigmoid)
-            if t != VECTOR_DEN_TILE:
-                nc.scalar.copy(den_window[t][:, 0:S], u_bank[:])
+            nc.scalar.copy(logit[t][:, 0:S], u_bank[:])
 
         def project_prices(t):
             y_bank = bank(4 + t, "y_bank%d" % t)
@@ -148,19 +156,21 @@ def tile_picked_vwap3_none_po_kernel(
             nc.vector.scalar_tensor_tensor(traded[t][:, 0:S], y_bank[:], gain[:, t : t + 1], volume(t), MULT, MULT)
 
         project_volumes(0)
+        w.setdefault(0, sbuf("w1", [P, 2 * H], U8, "w2_first"))
+        deal_by_runs(w[0][:], raw_w[0], 8, 0, TILES)
         ws.setdefault(0, sbuf("ws1", [P, H], U8, "ws2_first"))
         deal_by_runs(ws[0][:], raw_s[0], 4, 0, TILES)
-        nc.sync.dma_start(out=raw_w[0][:].bitcast(I32), in_=w3_words[0].bitcast(I32))
         load_scale_rows(raw_s[0], w3_scales, nc.sync)
+        w.setdefault(2, sbuf("w3", [P, 2 * H], U8, "raw_w0"))
+        nc.vector.tensor_copy(
+            out=w[2][:].rearrange("p (t m b) -> p t m b", t=TILES, b=2),
+            in_=raw_w[1][:].rearrange("p (m t b) -> p t m b", t=TILES, b=2),
+        )
         for t in range(1, TILES):
             project_volumes(t)
             project_prices(t - 1)
         project_prices(TILES - 1)
 
-        nc.vector.tensor_copy(
-            out=w[2][:].rearrange("p (t m b) -> p t m b", t=TILES, b=2),
-            in_=raw_w[0][:].rearrange("p (m t b) -> p t m b", t=TILES, b=2),
-        )
         nc.vector.tensor_copy(
             out=ws[2][:].rearrange("p (t m) -> p t m", t=TILES),
             in_=raw_s[0][:].rearrange("p (m t) -> p t m", t=TILES),
@@ -184,10 +194,10 @@ def tile_picked_vwap3_none_po_kernel(
         def pick_volumes(t):
             got = sbuf("den_%d" % t, [P, 3, S], F32)
             for l in range(3):
-                if t == VECTOR_DEN_TILE:
-                    nc.vector.tensor_copy(out=got[:, l, :], in_=den_window[t][:].indirect(picks[l][:]))
+                if t == VECTOR_DEN_TILE and l < 2:
+                    nc.vector.tensor_copy(out=got[:, l, :], in_=volumes[t][:].indirect(picks[l][:]))
                 else:
-                    nc.scalar.activation(got[:, l, :], den_window[t][:].indirect(picks[l][:]), ACT.Sigmoid)
+                    nc.scalar.activation(got[:, l, :], logit[t][:].indirect(picks[l][:]), ACT.Sigmoid)
             add_turned(den, t, got, range(BLOCKS))
 
         def pick_traded(t, blocks, slot=None):
@@ -198,11 +208,12 @@ def tile_picked_vwap3_none_po_kernel(
             add_turned(num, t, got, blocks)
 
         pick_traded(0, (0, 1, 2, 3))
-        for t in (0, VECTOR_DEN_TILE, 1, 2):
+        for t in (0, 1, VECTOR_DEN_TILE, 2):
             pick_volumes(t)
         pick_traded(1, (0, 1, 2, 3))
-        pick_traded(2, (0, 1))
+        pick_traded(2, (0, 1, 2, 3))
         pick_traded(3, (0, 1))
+        pick_traded(3, (2, 3))
 
         out_words = sbuf("out_words", [P, S], I32)
         out_scales = sbuf("out_scales", [P, S], U8)
@@ -215,16 +226,18 @@ def tile_picked_vwap3_none_po_kernel(
         def as_runs(tile):
             return tile[:].rearrange("j (g t i) -> j g t i", t=TILES, i=16)
 
+        inverse = []
         for jb in range(BLOCKS):
-            cols = slice(P * jb, P * (jb + 1))
             root = sbuf("root%d" % jb, [P, H], F32)
             nc.scalar.activation(as_runs(root), in_feature_order(den[jb]), ACT.Abs_reciprocal_sqrt)
             inv = sbuf("inv%d" % jb, [P, H], F32)
             nc.scalar.activation(inv[:], root[:], ACT.Square)
+            inverse.append(inv)
+
+        for jb in range(BLOCKS):
+            cols = slice(P * jb, P * (jb + 1))
             z_t = sbuf("z_t%d" % jb, [P, H], BF16)
-            nc.vector.tensor_tensor(as_runs(z_t), in_feature_order(num[jb]), as_runs(inv), MULT)
-            if jb < 2:
-                pick_traded(2 + jb, (2, 3), "inv%d" % jb)
+            nc.vector.tensor_tensor(as_runs(z_t), in_feature_order(num[jb]), as_runs(inverse[jb]), MULT)
             z_bank = bank(jb, "z_bank%d" % jb)
             for u in range(2):
                 nc.tensor.transpose(z_bank[:, P * u : P * (u + 1)], z_t[:].bitcast(F32)[:, u : H // 2 : 2], ident[:])

@@ -16,6 +16,7 @@ FP8X4 = mybir.dt.float8_e4m3fn_x4
 FP4X4 = mybir.dt.float4_e2m1fn_x4
 ACT = mybir.ActivationFunctionType
 MULT = mybir.AluOpType.mult
+ADD = mybir.AluOpType.add
 
 P = 128
 TILES = 4
@@ -179,14 +180,14 @@ def tile_picked_vwap3_none_po_kernel(
         den = [bank(jb, "den%d" % jb) for jb in range(BLOCKS)]
         num = [bank(4 + jb, "num%d" % jb) for jb in range(BLOCKS)]
 
-        def add_turned(banks, t, got, blocks):
+        def add_turned(banks, t, got, blocks, first=0):
             for n, jb in enumerate(blocks):
-                for l in range(3):
+                for l in range(first, 3):
                     nc.tensor.matmul(
                         banks[jb][:, P * t : P * (t + 1)],
                         got[:, l, P * n : P * (n + 1)],
                         ident[:],
-                        start=(l == 0),
+                        start=(l == first),
                         stop=(l == 2),
                         is_transpose=True,
                     )
@@ -204,8 +205,11 @@ def tile_picked_vwap3_none_po_kernel(
             got = sbuf("num_%d_%d" % (t, blocks[0]), [P, 3, P * len(blocks)], F32, slot)
             for l in range(3):
                 index = picks[l][:, 8 * blocks[0] : 8 * (blocks[-1] + 1)]
-                nc.vector.tensor_copy(out=got[:, l, :], in_=traded[t][:].indirect(index))
-            add_turned(num, t, got, blocks)
+                if l < 2:
+                    nc.vector.tensor_copy(out=got[:, l, :], in_=traded[t][:].indirect(index))
+                else:
+                    nc.vector.tensor_tensor(got[:, l, :], traded[t][:].indirect(index), got[:, 0, :], ADD)
+            add_turned(num, t, got, blocks, 1)
 
         pick_traded(0, (0, 1, 2, 3))
         for t in (0, 1, VECTOR_DEN_TILE, 2):

from contextlib import ExitStack

import concourse.mybir as mybir
from concourse.masks import make_identity

K, T, S, N, H = 512, 2048, 512, 512, 512
FLOPS = 2 * K * H * S * 2 + 2 * H * N * S

F32 = mybir.dt.float32
BF16 = mybir.dt.bfloat16
I32 = mybir.dt.int32
U32 = mybir.dt.uint32
U16 = mybir.dt.uint16
U8 = mybir.dt.uint8
FP8X4 = mybir.dt.float8_e4m3fn_x4
FP4X4 = mybir.dt.float4_e2m1fn_x4
ACT = mybir.ActivationFunctionType
MULT = mybir.AluOpType.mult
ADD = mybir.AluOpType.add

P = 128
TILES = 4
BLOCKS = S // P
HALF = S // 2
VECTOR_DEN_TILE = 3


def tile_picked_vwap3_none_po_kernel(
    tc, x_words, x_scales, w1_words, w1_scales, w2_words, w2_scales, gn, w3_words, w3_scales,
    offs, two, b1, b3, b4, out_0, out_1, out_2,
):
    nc = tc.nc
    with ExitStack() as ctx:
        lists = ctx.enter_context(tc.tile_pool(name="lists", bufs=1))
        sb = ctx.enter_context(tc.tile_pool(name="sb", bufs=1))
        ps = ctx.enter_context(tc.psum_pool(name="ps", bufs=1))

        def sbuf(name, shape, dtype, slot=None):
            return sb.tile(shape, dtype, name=name, tag=slot or name, align_bytes=64)

        def bank(b, name):
            return ps.tile([P, 512], F32, name=name, tag="bank%d" % b)

        def load_list(name, src):
            held = lists.tile([P, S // 16], U16, name=name)
            nc.sync.dma_start(held[:], src)
            return held

        def load_scale_rows(plane, scales, queue):
            for q in range(4):
                (queue if q % 2 else nc.sync).dma_start(
                    out=plane[32 * q : 32 * q + 4, :].bitcast(I32), in_=scales[0, 4 * q : 4 * q + 4, :].bitcast(I32)
                )

        xw = sbuf("xw", [P, T], I32)
        xs = sbuf("xs", [P, T], U8)
        raw_w = [sbuf("raw_w%d" % i, [P, 2 * H], U8) for i in range(2)]
        raw_s = [sbuf("raw_s%d" % i, [P, H], U8) for i in range(2)]
        gn_rows = sbuf("gn_rows", [P, P], F32)
        ident = sbuf("ident", [P, P], F32)

        nc.vector.memset(xs[:].bitcast(I32), 0)
        nc.vector.memset(gn_rows[:], 0.0)
        nc.vector.memset(raw_s[1][:].bitcast(I32), 0)
        nc.vector.memset(raw_s[0][:].bitcast(I32), 0)
        make_identity(nc, ident[:])

        two_t = load_list("two_t", two)
        offs_t = load_list("offs_t", offs)
        nc.sync.dma_start(out=raw_w[1][:].bitcast(I32), in_=w2_words[0].bitcast(I32))
        load_scale_rows(xs, x_scales, nc.sync)
        nc.sync.dma_start(out=xw[:], in_=x_words[0].rearrange("p c r -> p (c r)").bitcast(I32))
        nc.sync.dma_start(
            out=gn_rows[0:TILES, :].rearrange("t (g i) -> t g i", i=16),
            in_=gn.rearrange("(g t i) o -> t g (i o)", t=TILES, i=16),
        )
        load_scale_rows(raw_s[1], w2_scales, nc.sync)
        nc.sync.dma_start(out=raw_w[0][:].bitcast(I32), in_=w1_words[0].bitcast(I32))
        load_scale_rows(raw_s[0], w1_scales, nc.sync)
        picks = [load_list(name, src) for name, src in (("b1_t", b1), ("b3_t", b3), ("b4_t", b4))]

        gn_bank = bank(7, "gn_bank")
        nc.tensor.transpose(gn_bank[:, 0:P], gn_rows[:], ident[:])
        gain = sbuf("gain", [P, TILES], F32)
        nc.vector.tensor_copy(out=gain[:], in_=gn_bank[:, 0:TILES])

        w2_first = sbuf("w2_first", [P, 2 * P], U8)
        w2_rest = sbuf("w2_rest", [P, 2 * (H - P)], U8)
        ws2_first = sbuf("ws2_first", [P, P], U8)
        ws2_rest = sbuf("ws2_rest", [P, H - P], U8)

        def deal_by_runs(dst, src, words, t0, t1):
            nc.vector.tensor_copy(
                out=dst.bitcast(I32).rearrange("p (t g k) -> p t g k", t=t1 - t0, k=words),
                in_=src[:].bitcast(I32).rearrange("p (g t k) -> p t g k", t=TILES, k=words)[:, t0:t1],
            )

        def pick_scales(name, index, slot=None):
            got = sbuf(name, [P, S], U8, slot)
            nc.vector.tensor_copy(out=got[:], in_=xs[:].indirect(index[:]))
            return got

        def pick_words(name, index, slot=None):
            got = sbuf(name, [P, S], U32, slot)
            nc.vector.tensor_copy(out=got[:], in_=xw[:].bitcast(U32).indirect(index[:]))
            return got

        def weight_scales(i, t):
            if i != 1:
                return ws[i][:, P * t : P * (t + 1)]
            return ws2_first[:] if t == 0 else ws2_rest[:, P * (t - 1) : P * t]

        def weight_words(i, t):
            if i != 1:
                return w[i][:, 2 * P * t : 2 * P * (t + 1)]
            return w2_first[:] if t == 0 else w2_rest[:, 2 * P * (t - 1) : 2 * P * t]

        def product(out, i, t, codes, scales):
            nc.tensor.matmul_mx(
                out=out,
                lhsT=weight_words(i, t).bitcast(FP4X4),
                lhsT_scale=weight_scales(i, t),
                rhs=codes.bitcast(FP8X4),
                rhs_scale=scales,
                start=True,
                stop=True,
            )

        two_s = pick_scales("two_s", two_t)
        two_w = pick_words("two_w", two_t)
        deal_by_runs(w2_first[:], raw_w[1], 8, 0, 1)
        deal_by_runs(w2_rest[:], raw_w[1], 8, 1, TILES)
        deal_by_runs(ws2_first[:], raw_s[1], 4, 0, 1)
        deal_by_runs(ws2_rest[:], raw_s[1], 4, 1, TILES)
        offs_s = pick_scales("offs_s", offs_t)
        offs_w = pick_words("offs_w", offs_t, "raw_s1")
        nc.sync.dma_start(out=raw_w[1][:].bitcast(I32), in_=w3_words[0].bitcast(I32))
        w = {}
        ws = {2: sbuf("ws3", [P, H], U8)}

        logit = [sbuf("logit%d" % t, [P, 2 * S], F32) for t in range(TILES)]
        volumes = [sbuf("volume%d" % t, [P, 2 * S], F32) for t in range(TILES)]
        traded = [sbuf("traded%d" % t, [P, 2 * S], F32) for t in range(TILES)]

        def volume(t):
            return volumes[t][:, 0:S]

        def project_volumes(t):
            u_bank = bank(t % 2, "u_bank%d" % t)
            product(u_bank[:], 1, t, two_w[:], two_s[:])
            nc.scalar.activation(volume(t), u_bank[:], ACT.Sigmoid)
            nc.scalar.copy(logit[t][:, 0:S], u_bank[:])

        def project_prices(t):
            y_bank = bank(4 + t, "y_bank%d" % t)
            product(y_bank[:], 0, t, offs_w[:], offs_s[:])
            nc.vector.scalar_tensor_tensor(traded[t][:, 0:S], y_bank[:], gain[:, t : t + 1], volume(t), MULT, MULT)

        project_volumes(0)
        w.setdefault(0, sbuf("w1", [P, 2 * H], U8, "w2_first"))
        deal_by_runs(w[0][:], raw_w[0], 8, 0, TILES)
        ws.setdefault(0, sbuf("ws1", [P, H], U8, "ws2_first"))
        deal_by_runs(ws[0][:], raw_s[0], 4, 0, TILES)
        load_scale_rows(raw_s[0], w3_scales, nc.sync)
        w.setdefault(2, sbuf("w3", [P, 2 * H], U8, "raw_w0"))
        nc.vector.tensor_copy(
            out=w[2][:].rearrange("p (t m b) -> p t m b", t=TILES, b=2),
            in_=raw_w[1][:].rearrange("p (m t b) -> p t m b", t=TILES, b=2),
        )
        for t in range(1, TILES):
            project_volumes(t)
            project_prices(t - 1)
        project_prices(TILES - 1)

        nc.vector.tensor_copy(
            out=ws[2][:].rearrange("p (t m) -> p t m", t=TILES),
            in_=raw_s[0][:].rearrange("p (m t) -> p t m", t=TILES),
        )

        den = [bank(jb, "den%d" % jb) for jb in range(BLOCKS)]
        num = [bank(4 + jb, "num%d" % jb) for jb in range(BLOCKS)]

        def add_turned(banks, t, got, blocks, first=0):
            for n, jb in enumerate(blocks):
                for l in range(first, 3):
                    nc.tensor.matmul(
                        banks[jb][:, P * t : P * (t + 1)],
                        got[:, l, P * n : P * (n + 1)],
                        ident[:],
                        start=(l == first),
                        stop=(l == 2),
                        is_transpose=True,
                    )

        def pick_volumes(t):
            got = sbuf("den_%d" % t, [P, 3, S], F32)
            for l in range(3):
                if t == VECTOR_DEN_TILE and l < 2:
                    nc.vector.tensor_copy(out=got[:, l, :], in_=volumes[t][:].indirect(picks[l][:]))
                else:
                    nc.scalar.activation(got[:, l, :], logit[t][:].indirect(picks[l][:]), ACT.Sigmoid)
            add_turned(den, t, got, range(BLOCKS))

        def pick_traded(t, blocks, slot=None):
            got = sbuf("num_%d_%d" % (t, blocks[0]), [P, 3, P * len(blocks)], F32, slot)
            for l in range(3):
                index = picks[l][:, 8 * blocks[0] : 8 * (blocks[-1] + 1)]
                if l < 2:
                    nc.vector.tensor_copy(out=got[:, l, :], in_=traded[t][:].indirect(index))
                else:
                    nc.vector.tensor_tensor(got[:, l, :], traded[t][:].indirect(index), got[:, 0, :], ADD)
            add_turned(num, t, got, blocks, 1)

        pick_traded(0, (0, 1, 2, 3))
        for t in (0, 1, VECTOR_DEN_TILE, 2):
            pick_volumes(t)
        pick_traded(1, (0, 1, 2, 3))
        pick_traded(2, (0, 1, 2, 3))
        pick_traded(3, (0, 1))
        pick_traded(3, (2, 3))

        out_words = sbuf("out_words", [P, S], I32)
        out_scales = sbuf("out_scales", [P, S], U8)
        out_rows = out_0.rearrange("(p t) j -> p t j", t=TILES)
        out_codes = out_1[0].rearrange("p c r -> p (c r)").bitcast(I32)

        def in_feature_order(b):
            return b[:].rearrange("j (t g i) -> j g t i", t=TILES, i=16)

        def as_runs(tile):
            return tile[:].rearrange("j (g t i) -> j g t i", t=TILES, i=16)

        inverse = []
        for jb in range(BLOCKS):
            root = sbuf("root%d" % jb, [P, H], F32)
            nc.scalar.activation(as_runs(root), in_feature_order(den[jb]), ACT.Abs_reciprocal_sqrt)
            inv = sbuf("inv%d" % jb, [P, H], F32)
            nc.scalar.activation(inv[:], root[:], ACT.Square)
            inverse.append(inv)

        for jb in range(BLOCKS):
            cols = slice(P * jb, P * (jb + 1))
            z_t = sbuf("z_t%d" % jb, [P, H], BF16)
            nc.vector.tensor_tensor(as_runs(z_t), in_feature_order(num[jb]), as_runs(inverse[jb]), MULT)
            z_bank = bank(jb, "z_bank%d" % jb)
            for u in range(2):
                nc.tensor.transpose(z_bank[:, P * u : P * (u + 1)], z_t[:].bitcast(F32)[:, u : H // 2 : 2], ident[:])
            z = sbuf("z%d" % jb, [P, 4 * P], BF16)
            nc.scalar.copy(
                z[:].bitcast(F32).rearrange("p (j u) -> p j u", u=2),
                z_bank[:, 0 : 2 * P].rearrange("p (u j) -> p j u", u=2),
            )
            z_words = sbuf("z_words%d" % jb, [P, P], U32)
            z_scales = sbuf("z_scales%d" % jb, [P, P], U8)
            nc.vector.quantize_mx(out=z_words[:].bitcast(FP8X4), scales=z_scales[:], in_=z[:])
            o_bank = bank(4 + jb, "o_bank%d" % jb)
            for t in range(TILES):
                product(o_bank[:, P * t : P * (t + 1)], 2, t, z_words[:], z_scales[:])
            o = sbuf("o%d" % jb, [P, TILES, P], F32)
            nc.scalar.copy(o[:].rearrange("p t j -> p (t j)"), o_bank[:])
            nc.sync.dma_start(out=out_rows[:, :, cols], in_=o[:])
            o16 = sbuf("o16_%d" % jb, [P, P, TILES], BF16)
            nc.vector.tensor_copy(out=o16[:], in_=o[:].rearrange("p t j -> p j t"))
            nc.vector.quantize_mx(
                out=out_words[:, cols].bitcast(FP8X4), scales=out_scales[:, cols], in_=o16[:].rearrange("p j t -> p (j t)")
            )
            nc.sync.dma_start(out=out_codes[:, cols], in_=out_words[:, cols])
        for q in range(4):
            queue = nc.scalar if q % 2 else nc.sync
            queue.dma_start(out=out_2[0, 4 * q : 4 * q + 4, :].bitcast(I32), in_=out_scales[32 * q : 32 * q + 4, :].bitcast(I32))
